import numpy as np
import ml_dtypes


def mxq(x, axis, fmt="e4m3"):
    dtype, down = {"e4m3": (ml_dtypes.float8_e4m3fn, 7), "e5m2": (ml_dtypes.float8_e5m2, 14)}[fmt]
    v = np.moveaxis(np.asarray(x, np.float32).astype(ml_dtypes.bfloat16).astype(np.float64), axis, -1)
    blocks = v.reshape(v.shape[:-1] + (-1, 32))
    amax = np.abs(blocks).max(-1, keepdims=True)
    byte = np.maximum(np.where(amax > 0, np.frexp(amax)[1] - 1 + 127, 0) - down, 1)
    scale = np.exp2(byte - 127.0)
    codes = (blocks / scale).astype(np.float32).astype(dtype).astype(np.float64)
    return np.moveaxis((codes * scale).reshape(v.shape), -1, axis)


WIDE = False


def mx_kscale(k):
    if not WIDE:
        return np.ones(k)
    levels = np.array([18, -18])
    if k % 512:
        return np.exp2(np.random.permutation(np.resize(levels, k // 32))).repeat(32)
    a = np.empty((k // 512, 16))
    for p in range(k // 512):
        a[p, :8] = np.random.permutation(np.resize(levels, 8))
        for g in range(8):
            far = levels[np.abs(levels - a[p, g]) >= 10]
            a[p, g + 8] = far[np.random.randint(len(far))]
    return np.exp2(a.ravel()).repeat(32)


def f64(x):
    return np.asarray(x).astype(np.float64)


def striped(idx):
    return np.tile(np.asarray(idx).reshape(-1, 16).T, (8, 1)).astype(np.uint16)


def unstriped(offs):
    return offs[:16].T.reshape(-1).astype(np.int64)


B, N, T, D, DV, NQ = 2, 512, 2048, 512, 0, 512
PAGE = 32


def setup_inputs():
    n = np.random.standard_normal
    pages = np.random.permutation(T // PAGE)[:B * N // PAGE]
    idx = (pages[:, None] * PAGE + np.arange(PAGE)[None, :]).reshape(-1)
    z = mx_kscale(NQ)[:, None]
    return {
        "g": (n((B, NQ, N)) * z / np.sqrt(NQ)).astype(np.float32),
        "qm": (n((B, NQ, D)) / z).astype(np.float32),
        "offs": striped(idx),
    }


def reference(g, qm, offs):
    idx = unstriped(offs)
    dk = mxq(f64(qm), 1, "e4m3").transpose(0, 2, 1) @ mxq(f64(g), 1, "e5m2")
    out = np.zeros((D, T))
    out[:, idx] = dk.transpose(1, 0, 2).reshape(D, B * N)
    return out

@@ -1,0 +1,128 @@
+from contextlib import ExitStack
+
+import concourse.mybir as mybir
+
+B, NQ, NSLOT, D, T = 2, 512, 512, 512, 2048
+P = 128
+FLOPS = 2 * B * NQ * NSLOT * D
+
+F32 = mybir.dt.float32
+BF16 = mybir.dt.bfloat16
+U32 = mybir.dt.uint32
+U16 = mybir.dt.uint16
+U8 = mybir.dt.uint8
+E4M3 = mybir.dt.float8_e4m3fn_x4
+E5M2 = mybir.dt.float8_e5m2_x4
+
+
+def tile_attend_dk_kernel(tc, g, qm, offs, out):
+    nc = tc.nc
+    with ExitStack() as ctx:
+        held = ctx.enter_context(tc.tile_pool(name="held", bufs=1))
+        psum = ctx.enter_context(tc.psum_pool(name="psum", bufs=1))
+
+        def tile(shape, dtype, name):
+            return held.tile(shape, dtype, name=name, align_bytes=64)
+
+        offsets = held.tile([P, B * NSLOT // 16], U16, name="offsets")
+
+        def load(raw, src):
+            nc.sync.dma_start(out=raw, in_=src.rearrange("(p j) w -> p j w", j=4))
+
+        def interleave(copy, grouped, raw, c0, c1):
+            copy(out=grouped[:, c0:c1, :], in_=raw[:, :, c0:c1].rearrange("p j w -> p w j"))
+
+        def quantise(codes, scales, fmt, grouped):
+            nc.vector.quantize_mx(out=codes.bitcast(fmt), scales=scales, in_=grouped.rearrange("p w j -> p (w j)"))
+
+        pieces = [(0, 128), (128, 256), (256, 512)]
+        q_raw = [[tile([P, 4, c1 - c0], F32, "q_raw_%d_%d" % (k, b)) for b in range(B)] for k, (c0, c1) in enumerate(pieces)]
+        q_grp = [tile([P, B * (c1 - c0), 4], BF16, "q_grp_%d" % k) for k, (c0, c1) in enumerate(pieces)]
+        q_codes = [tile([P, B * (c1 - c0)], U32, "q_codes_%d" % k) for k, (c0, c1) in enumerate(pieces)]
+        q_scales = [tile([P, B * (c1 - c0)], U8, "q_scales_%d" % k) for k, (c0, c1) in enumerate(pieces)]
+        g0_raw = tile([P, 4, NSLOT], F32, "g0_raw")
+        g1_raw = [tile([P, 4, NSLOT // 2], F32, "g1_raw_%d" % h) for h in range(2)]
+        g_grp = [tile([P, NSLOT, 4], BF16, "g_grp_%d" % b) for b in range(B)]
+        g_codes = [tile([P, NSLOT], U32, "g_codes_%d" % b) for b in range(B)]
+        g_scales = [tile([P, NSLOT], U8, "g_scales_%d" % b) for b in range(B)]
+        windows = [tile([P, T], F32, "window_%d" % m) for m in range(D // P)]
+
+        def load_piece(k):
+            c0, c1 = pieces[k]
+            for b in range(B):
+                load(q_raw[k][b][:], qm[b, :, c0:c1])
+
+        load_piece(0)
+        load(g0_raw[:], g[0, :, :])
+        nc.sync.dma_start(offsets[:], offs)
+        for h in range(2):
+            load(g1_raw[h][:], g[1, :, h * 256:h * 256 + 256])
+        load_piece(1)
+        load_piece(2)
+
+        for m in range(D // P):
+            nc.vector.memset(windows[m][:], 0.0)
+
+        v = nc.vector.tensor_copy
+        s = nc.scalar.copy
+
+        def group_q(copy, k, b, c0, c1):
+            w = pieces[k][1] - pieces[k][0]
+            copy(out=q_grp[k][:, b * w + c0:b * w + c1, :], in_=q_raw[k][b][:, :, c0:c1].rearrange("p j w -> p w j"))
+
+        def product(m, b):
+            k = min(m, 2)
+            w = pieces[k][1] - pieces[k][0]
+            c0 = b * w + m * P - pieces[k][0]
+            acc = psum.tile([P, NSLOT], F32, name="acc_%d_%d" % (m, b))
+            nc.tensor.matmul_mx(
+                out=acc[:],
+                lhsT=q_codes[k][:, c0:c0 + P].bitcast(E4M3),
+                lhsT_scale=q_scales[k][:, c0:c0 + P],
+                rhs=g_codes[b][:].bitcast(E5M2),
+                rhs_scale=g_scales[b][:],
+                start=True,
+                stop=True,
+            )
+            return acc
+
+        def place(m, b, acc):
+            vals = tile([P, NSLOT], F32, "vals_%d_%d" % (m, b))
+            nc.scalar.copy(out=vals[:], in_=acc[:])
+            nc.vector.tensor_copy(windows[m][:].indirect(offsets[:, b * 32:b * 32 + 32]), vals[:])
+
+        def store(m):
+            nc.sync.dma_start(out=out[m * P:m * P + P, :], in_=windows[m][:])
+
+        group_q(s, 0, 0, 0, 128)
+        group_q(s, 0, 1, 0, 128)
+        interleave(v, g_grp[0], g0_raw, 0, 320)
+        interleave(s, g_grp[0], g0_raw, 320, 512)
+        quantise(q_codes[0][:], q_scales[0][:], E4M3, q_grp[0][:])
+        quantise(g_codes[0][:], g_scales[0][:], E5M2, g_grp[0][:])
+        acc00 = product(0, 0)
+        for h in range(2):
+            v(out=g_grp[1][:, h * 256:h * 256 + 160, :], in_=g1_raw[h][:, :, 0:160].rearrange("p j w -> p w j"))
+            s(out=g_grp[1][:, h * 256 + 160:h * 256 + 256, :], in_=g1_raw[h][:, :, 160:256].rearrange("p j w -> p w j"))
+        for h in range(2):
+            cols = slice(h * 256, h * 256 + 256)
+            quantise(g_codes[1][:, cols], g_scales[1][:, cols], E5M2, g_grp[1][:, cols, :])
+        place(0, 0, acc00)
+        place(0, 1, product(0, 1))
+        store(0)
+        group_q(v, 1, 0, 0, 128)
+        group_q(s, 1, 1, 0, 128)
+        quantise(q_codes[1][:], q_scales[1][:], E4M3, q_grp[1][:])
+        for b in range(B):
+            place(1, b, product(1, b))
+        store(1)
+        group_q(v, 2, 0, 0, 256)
+        group_q(s, 2, 1, 128, 256)
+        group_q(v, 2, 1, 0, 128)
+        for b in range(B):
+            cols = slice(b * 256, b * 256 + 256)
+            quantise(q_codes[2][:, cols], q_scales[2][:, cols], E4M3, q_grp[2][:, cols, :])
+        for m in (2, 3):
+            for b in range(B):
+                place(m, b, product(m, b))
+            store(m)

@@ -37,92 +37,110 @@ def tile_attend_dk_kernel(tc, g, qm, offs, out):
 
         pieces = [(0, 128), (128, 256), (256, 512)]
         q_raw = [[tile([P, 4, c1 - c0], F32, "q_raw_%d_%d" % (k, b)) for b in range(B)] for k, (c0, c1) in enumerate(pieces)]
-        q_grp = [tile([P, B * (c1 - c0), 4], BF16, "q_grp_%d" % k) for k, (c0, c1) in enumerate(pieces)]
-        q_codes = [tile([P, B * (c1 - c0)], U32, "q_codes_%d" % k) for k, (c0, c1) in enumerate(pieces)]
-        q_scales = [tile([P, B * (c1 - c0)], U8, "q_scales_%d" % k) for k, (c0, c1) in enumerate(pieces)]
-        g0_raw = tile([P, 4, NSLOT], F32, "g0_raw")
-        g1_raw = [tile([P, 4, NSLOT // 2], F32, "g1_raw_%d" % h) for h in range(2)]
+        q_grp = [[tile([P, c1 - c0, 4], BF16, "q_grp_%d_%d" % (k, b)) for b in range(B)] for k, (c0, c1) in enumerate(pieces)]
+        q_codes = [[tile([P, c1 - c0], U32, "q_codes_%d_%d" % (k, b)) for b in range(B)] for k, (c0, c1) in enumerate(pieces)]
+        q_scales = [[tile([P, c1 - c0], U8, "q_scales_%d_%d" % (k, b)) for b in range(B)] for k, (c0, c1) in enumerate(pieces)]
+        spans = [[(0, 512)], [(0, 256), (256, 512)]]
+        g_raw = [[tile([P, 4, c1 - c0], F32, "g_raw_%d_%d" % (b, h)) for h, (c0, c1) in enumerate(spans[b])] for b in range(B)]
         g_grp = [tile([P, NSLOT, 4], BF16, "g_grp_%d" % b) for b in range(B)]
         g_codes = [tile([P, NSLOT], U32, "g_codes_%d" % b) for b in range(B)]
         g_scales = [tile([P, NSLOT], U8, "g_scales_%d" % b) for b in range(B)]
         windows = [tile([P, T], F32, "window_%d" % m) for m in range(D // P)]
 
-        def load_piece(k):
+        def load_g(b, h):
+            c0, c1 = spans[b][h]
+            load(g_raw[b][h][:], g[b, :, c0:c1])
+
+        def load_q(k, b):
             c0, c1 = pieces[k]
-            for b in range(B):
-                load(q_raw[k][b][:], qm[b, :, c0:c1])
+            load(q_raw[k][b][:], qm[b, :, c0:c1])
 
-        load_piece(0)
-        load(g0_raw[:], g[0, :, :])
-        nc.sync.dma_start(offsets[:], offs)
-        for h in range(2):
-            load(g1_raw[h][:], g[1, :, h * 256:h * 256 + 256])
-        load_piece(1)
-        load_piece(2)
+        def quantise_g(b, h):
+            c0, c1 = spans[b][h]
+            quantise(g_codes[b][:, c0:c1], g_scales[b][:, c0:c1], E5M2, g_grp[b][:, c0:c1, :])
 
-        for m in range(D // P):
-            nc.vector.memset(windows[m][:], 0.0)
+        def group_g(b, h, n):
+            c0, c1 = spans[b][h]
+            raw = g_raw[b][h]
+            nc.vector.tensor_copy(out=g_grp[b][:, c0:c0 + n, :], in_=raw[:, :, 0:n].rearrange("p j w -> p w j"))
+            nc.scalar.copy(out=g_grp[b][:, c0 + n:c1, :], in_=raw[:, :, n:c1 - c0].rearrange("p j w -> p w j"))
 
-        v = nc.vector.tensor_copy
-        s = nc.scalar.copy
-
-        def group_q(copy, k, b, c0, c1):
+        def group_q(k, b, n):
             w = pieces[k][1] - pieces[k][0]
-            copy(out=q_grp[k][:, b * w + c0:b * w + c1, :], in_=q_raw[k][b][:, :, c0:c1].rearrange("p j w -> p w j"))
+            if n:
+                nc.vector.tensor_copy(out=q_grp[k][b][:, 0:n, :], in_=q_raw[k][b][:, :, 0:n].rearrange("p j w -> p w j"))
+            if n < w:
+                nc.scalar.copy(out=q_grp[k][b][:, n:w, :], in_=q_raw[k][b][:, :, n:w].rearrange("p j w -> p w j"))
+
+        def quantise_q(k, b):
+            quantise(q_codes[k][b][:], q_scales[k][b][:], E4M3, q_grp[k][b][:])
+
+        accs = {}
 
         def product(m, b):
             k = min(m, 2)
-            w = pieces[k][1] - pieces[k][0]
-            c0 = b * w + m * P - pieces[k][0]
+            c0 = m * P - pieces[k][0]
             acc = psum.tile([P, NSLOT], F32, name="acc_%d_%d" % (m, b))
             nc.tensor.matmul_mx(
                 out=acc[:],
-                lhsT=q_codes[k][:, c0:c0 + P].bitcast(E4M3),
-                lhsT_scale=q_scales[k][:, c0:c0 + P],
+                lhsT=q_codes[k][b][:, c0:c0 + P].bitcast(E4M3),
+                lhsT_scale=q_scales[k][b][:, c0:c0 + P],
                 rhs=g_codes[b][:].bitcast(E5M2),
                 rhs_scale=g_scales[b][:],
                 start=True,
                 stop=True,
             )
-            return acc
+            accs[m, b] = acc
 
-        def place(m, b, acc):
+        def place(m, b):
             vals = tile([P, NSLOT], F32, "vals_%d_%d" % (m, b))
-            nc.scalar.copy(out=vals[:], in_=acc[:])
+            nc.scalar.copy(out=vals[:], in_=accs[m, b][:])
             nc.vector.tensor_copy(windows[m][:].indirect(offsets[:, b * 32:b * 32 + 32]), vals[:])
 
         def store(m):
             nc.sync.dma_start(out=out[m * P:m * P + P, :], in_=windows[m][:])
 
-        group_q(s, 0, 0, 0, 128)
-        group_q(s, 0, 1, 0, 128)
-        interleave(v, g_grp[0], g0_raw, 0, 320)
-        interleave(s, g_grp[0], g0_raw, 320, 512)
-        quantise(q_codes[0][:], q_scales[0][:], E4M3, q_grp[0][:])
-        quantise(g_codes[0][:], g_scales[0][:], E5M2, g_grp[0][:])
-        acc00 = product(0, 0)
-        for h in range(2):
-            v(out=g_grp[1][:, h * 256:h * 256 + 160, :], in_=g1_raw[h][:, :, 0:160].rearrange("p j w -> p w j"))
-            s(out=g_grp[1][:, h * 256 + 160:h * 256 + 256, :], in_=g1_raw[h][:, :, 160:256].rearrange("p j w -> p w j"))
-        for h in range(2):
-            cols = slice(h * 256, h * 256 + 256)
-            quantise(g_codes[1][:, cols], g_scales[1][:, cols], E5M2, g_grp[1][:, cols, :])
-        place(0, 0, acc00)
-        place(0, 1, product(0, 1))
+        load_g(0, 0)
+        load_q(0, 0)
+        load_g(1, 0)
+        load_g(1, 1)
+        load_q(0, 1)
+        load_q(1, 0)
+        nc.sync.dma_start(offsets[:], offs)
+        load_q(1, 1)
+        load_q(2, 0)
+        load_q(2, 1)
+        for m in range(D // P):
+            nc.vector.memset(windows[m][:], 0.0)
+
+        group_q(0, 0, 0)
+        group_g(0, 0, 320)
+        quantise_q(0, 0)
+        quantise_g(0, 0)
+        product(0, 0)
+        group_g(1, 0, 160)
+        group_q(0, 1, 64)
+        quantise_g(1, 0)
+        quantise_q(0, 1)
+        group_g(1, 1, 160)
+        quantise_g(1, 1)
+        product(0, 1)
+        place(0, 0)
+        for b in range(B):
+            group_q(1, b, 0)
+            quantise_q(1, b)
+        for b in range(B):
+            product(1, b)
+        place(0, 1)
         store(0)
-        group_q(v, 1, 0, 0, 128)
-        group_q(s, 1, 1, 0, 128)
-        quantise(q_codes[1][:], q_scales[1][:], E4M3, q_grp[1][:])
         for b in range(B):
-            place(1, b, product(1, b))
+            group_q(2, b, 128)
+            quantise_q(2, b)
+        for b in range(B):
+            place(1, b)
         store(1)
-        group_q(v, 2, 0, 0, 256)
-        group_q(s, 2, 1, 128, 256)
-        group_q(v, 2, 1, 0, 128)
-        for b in range(B):
-            cols = slice(b * 256, b * 256 + 256)
-            quantise(q_codes[2][:, cols], q_scales[2][:, cols], E4M3, q_grp[2][:, cols, :])
         for m in (2, 3):
             for b in range(B):
-                place(m, b, product(m, b))
+                product(m, b)
+                place(m, b)
             store(m)

@@ -62,15 +62,15 @@ def tile_attend_dk_kernel(tc, g, qm, offs, out):
         def group_g(b, h, n):
             c0, c1 = spans[b][h]
             raw = g_raw[b][h]
-            nc.vector.tensor_copy(out=g_grp[b][:, c0:c0 + n, :], in_=raw[:, :, 0:n].rearrange("p j w -> p w j"))
-            nc.scalar.copy(out=g_grp[b][:, c0 + n:c1, :], in_=raw[:, :, n:c1 - c0].rearrange("p j w -> p w j"))
+            nc.vector.tensor_copy(out=g_grp[b][:, c0:c0 + n, :].rearrange("p (c i) j -> p c j i", i=4), in_=raw[:, :, 0:n].rearrange("p j (c i) -> p c j i", i=4))
+            nc.scalar.copy(out=g_grp[b][:, c0 + n:c1, :].rearrange("p (c i) j -> p c j i", i=4), in_=raw[:, :, n:c1 - c0].rearrange("p j (c i) -> p c j i", i=4))
 
         def group_q(k, b, n):
             w = pieces[k][1] - pieces[k][0]
             if n:
-                nc.vector.tensor_copy(out=q_grp[k][b][:, 0:n, :], in_=q_raw[k][b][:, :, 0:n].rearrange("p j w -> p w j"))
+                nc.vector.tensor_copy(out=q_grp[k][b][:, 0:n, :].rearrange("p (c i) j -> p c j i", i=4), in_=q_raw[k][b][:, :, 0:n].rearrange("p j (c i) -> p c j i", i=4))
             if n < w:
-                nc.scalar.copy(out=q_grp[k][b][:, n:w, :], in_=q_raw[k][b][:, :, n:w].rearrange("p j w -> p w j"))
+                nc.scalar.copy(out=q_grp[k][b][:, n:w, :].rearrange("p (c i) j -> p c j i", i=4), in_=q_raw[k][b][:, :, n:w].rearrange("p j (c i) -> p c j i", i=4))
 
         def quantise_q(k, b):
             quantise(q_codes[k][b][:], q_scales[k][b][:], E4M3, q_grp[k][b][:])

@@ -29,17 +29,14 @@ def tile_attend_dk_kernel(tc, g, qm, offs, out):
         def load(raw, src):
             nc.sync.dma_start(out=raw, in_=src.rearrange("(p j) w -> p j w", j=4))
 
-        def interleave(copy, grouped, raw, c0, c1):
-            copy(out=grouped[:, c0:c1, :], in_=raw[:, :, c0:c1].rearrange("p j w -> p w j"))
-
         def quantise(codes, scales, fmt, grouped):
             nc.vector.quantize_mx(out=codes.bitcast(fmt), scales=scales, in_=grouped.rearrange("p w j -> p (w j)"))
 
         pieces = [(0, 128), (128, 256), (256, 512)]
         q_raw = [[tile([P, 4, c1 - c0], F32, "q_raw_%d_%d" % (k, b)) for b in range(B)] for k, (c0, c1) in enumerate(pieces)]
-        q_grp = [[tile([P, c1 - c0, 4], BF16, "q_grp_%d_%d" % (k, b)) for b in range(B)] for k, (c0, c1) in enumerate(pieces)]
-        q_codes = [[tile([P, c1 - c0], U32, "q_codes_%d_%d" % (k, b)) for b in range(B)] for k, (c0, c1) in enumerate(pieces)]
-        q_scales = [[tile([P, c1 - c0], U8, "q_scales_%d_%d" % (k, b)) for b in range(B)] for k, (c0, c1) in enumerate(pieces)]
+        q_grp = [tile([P, B, P, 4], BF16, "q_grp_%d" % k) for k in range(2)]
+        q_codes = [tile([P, B, P], U32, "q_codes_0"), held.tile([P, B, P], U32, name="q_codes_1", tag="shared", align_bytes=64), tile([P, B, 2 * P], U32, "q_codes_2")]
+        q_scales = [tile([P, B, c1 - c0], U8, "q_scales_%d" % k) for k, (c0, c1) in enumerate(pieces)]
         spans = [[(0, 512)], [(0, 256), (256, 512)]]
         g_raw = [[tile([P, 4, c1 - c0], F32, "g_raw_%d_%d" % (b, h)) for h, (c0, c1) in enumerate(spans[b])] for b in range(B)]
         g_grp = [tile([P, NSLOT, 4], BF16, "g_grp_%d" % b) for b in range(B)]
@@ -68,14 +65,15 @@ def tile_attend_dk_kernel(tc, g, qm, offs, out):
         def group_q(k, b, n):
             w = pieces[k][1] - pieces[k][0]
             if n:
-                nc.vector.tensor_copy(out=q_grp[k][b][:, 0:n, :].rearrange("p (c i) j -> p c j i", i=4), in_=q_raw[k][b][:, :, 0:n].rearrange("p j (c i) -> p c j i", i=4))
+                nc.vector.tensor_copy(out=q_grp[k][:, b, 0:n, :].rearrange("p (c i) j -> p c j i", i=4), in_=q_raw[k][b][:, :, 0:n].rearrange("p j (c i) -> p c j i", i=4))
             if n < w:
-                nc.scalar.copy(out=q_grp[k][b][:, n:w, :].rearrange("p (c i) j -> p c j i", i=4), in_=q_raw[k][b][:, :, n:w].rearrange("p j (c i) -> p c j i", i=4))
+                nc.scalar.copy(out=q_grp[k][:, b, n:w, :].rearrange("p (c i) j -> p c j i", i=4), in_=q_raw[k][b][:, :, n:w].rearrange("p j (c i) -> p c j i", i=4))
 
         def quantise_q(k, b):
-            quantise(q_codes[k][b][:], q_scales[k][b][:], E4M3, q_grp[k][b][:])
+            quantise(q_codes[k][:, b, :], q_scales[k][:, b, :], E4M3, q_grp[k][:, b, :, :])
 
         accs = {}
+        staged = {}
 
         def product(m, b):
             k = min(m, 2)
@@ -83,8 +81,8 @@ def tile_attend_dk_kernel(tc, g, qm, offs, out):
             acc = psum.tile([P, NSLOT], F32, name="acc_%d_%d" % (m, b))
             nc.tensor.matmul_mx(
                 out=acc[:],
-                lhsT=q_codes[k][b][:, c0:c0 + P].bitcast(E4M3),
-                lhsT_scale=q_scales[k][b][:, c0:c0 + P],
+                lhsT=q_codes[k][:, b, c0:c0 + P].bitcast(E4M3),
+                lhsT_scale=q_scales[k][:, b, c0:c0 + P],
                 rhs=g_codes[b][:].bitcast(E5M2),
                 rhs_scale=g_scales[b][:],
                 start=True,
@@ -92,55 +90,62 @@ def tile_attend_dk_kernel(tc, g, qm, offs, out):
             )
             accs[m, b] = acc
 
-        def place(m, b):
-            vals = tile([P, NSLOT], F32, "vals_%d_%d" % (m, b))
-            nc.scalar.copy(out=vals[:], in_=accs[m, b][:])
-            nc.vector.tensor_copy(windows[m][:].indirect(offsets[:, b * 32:b * 32 + 32]), vals[:])
+        def copy_out(m, b):
+            if b == 0:
+                staged[m] = tile([P, B, NSLOT], F32, "vals_%d" % m)
+            nc.scalar.copy(out=staged[m][:, b, :], in_=accs[m, b][:])
+
+        def scatter(m, b):
+            nc.vector.tensor_copy(windows[m][:].indirect(offsets[:, b * 32:b * 32 + 32]), staged[m][:, b, :])
+
+        def scatter_both(m):
+            nc.vector.tensor_copy(windows[m][:].indirect(offsets[:]), staged[m][:].rearrange("p b s -> p (b s)"))
 
         def store(m):
             nc.sync.dma_start(out=out[m * P:m * P + P, :], in_=windows[m][:])
 
         load_g(0, 0)
-        load_q(0, 0)
         load_g(1, 0)
-        load_g(1, 1)
+        load_q(0, 0)
         load_q(0, 1)
+        load_g(1, 1)
         load_q(1, 0)
-        nc.sync.dma_start(offsets[:], offs)
         load_q(1, 1)
+        nc.sync.dma_start(offsets[:], offs)
         load_q(2, 0)
         load_q(2, 1)
         for m in range(D // P):
             nc.vector.memset(windows[m][:], 0.0)
 
-        group_q(0, 0, 0)
         group_g(0, 0, 320)
-        quantise_q(0, 0)
-        quantise_g(0, 0)
-        product(0, 0)
         group_g(1, 0, 160)
-        group_q(0, 1, 64)
+        quantise_g(0, 0)
+        group_q(0, 0, 0)
+        quantise_q(0, 0)
+        product(0, 0)
         quantise_g(1, 0)
-        quantise_q(0, 1)
+        group_q(0, 1, 0)
         group_g(1, 1, 160)
+        quantise_q(0, 1)
         quantise_g(1, 1)
         product(0, 1)
-        place(0, 0)
+        copy_out(0, 0)
+        scatter(0, 0)
         for b in range(B):
-            group_q(1, b, 0)
+            group_q(1, b, 64)
             quantise_q(1, b)
-        for b in range(B):
             product(1, b)
-        place(0, 1)
+        copy_out(0, 1)
+        scatter(0, 1)
         store(0)
+        q_grp.append(held.tile([P, B, 2 * P, 4], BF16, name="q_grp_2", tag="shared", align_bytes=64))
         for b in range(B):
             group_q(2, b, 128)
             quantise_q(2, b)
-        for b in range(B):
-            place(1, b)
-        store(1)
-        for m in (2, 3):
+        for m in (1, 2, 3):
             for b in range(B):
-                product(m, b)
-                place(m, b)
+                if m > 1:
+                    product(m, b)
+                copy_out(m, b)
+            scatter_both(m)
             store(m)

@@ -8,6 +8,7 @@ FLOPS = 2 * B * NQ * NSLOT * D
 
 F32 = mybir.dt.float32
 BF16 = mybir.dt.bfloat16
+I32 = mybir.dt.int32
 U32 = mybir.dt.uint32
 U16 = mybir.dt.uint16
 U8 = mybir.dt.uint8
@@ -98,9 +99,6 @@ def tile_attend_dk_kernel(tc, g, qm, offs, out):
         def scatter(m, b):
             nc.vector.tensor_copy(windows[m][:].indirect(offsets[:, b * 32:b * 32 + 32]), staged[m][:, b, :])
 
-        def scatter_both(m):
-            nc.vector.tensor_copy(windows[m][:].indirect(offsets[:]), staged[m][:].rearrange("p b s -> p (b s)"))
-
         def store(m):
             nc.sync.dma_start(out=out[m * P:m * P + P, :], in_=windows[m][:])
 
@@ -115,37 +113,40 @@ def tile_attend_dk_kernel(tc, g, qm, offs, out):
         load_q(2, 0)
         load_q(2, 1)
         for m in range(D // P):
-            nc.vector.memset(windows[m][:], 0.0)
+            engine = nc.gpsimd if m == 3 else nc.vector
+            engine.memset(windows[m][:].bitcast(I32), 0)
 
-        group_g(0, 0, 320)
-        group_g(1, 0, 160)
+        group_g(0, 0, 256)
+        group_g(1, 0, 128)
         quantise_g(0, 0)
         group_q(0, 0, 0)
         quantise_q(0, 0)
         product(0, 0)
         quantise_g(1, 0)
         group_q(0, 1, 0)
-        group_g(1, 1, 160)
+        group_g(1, 1, 128)
         quantise_q(0, 1)
         quantise_g(1, 1)
         product(0, 1)
-        copy_out(0, 0)
-        scatter(0, 0)
         for b in range(B):
             group_q(1, b, 64)
+        copy_out(0, 0)
+        for b in range(B):
             quantise_q(1, b)
+        scatter(0, 0)
+        for b in range(B):
             product(1, b)
         copy_out(0, 1)
         scatter(0, 1)
         store(0)
         q_grp.append(held.tile([P, B, 2 * P, 4], BF16, name="q_grp_2", tag="shared", align_bytes=64))
         for b in range(B):
-            group_q(2, b, 128)
+            group_q(2, b, 256 - 256 * b)
             quantise_q(2, b)
         for m in (1, 2, 3):
             for b in range(B):
                 if m > 1:
                     product(m, b)
                 copy_out(m, b)
-            scatter_both(m)
+                scatter(m, b)
             store(m)

from contextlib import ExitStack

import concourse.mybir as mybir

B, NQ, NSLOT, D, T = 2, 512, 512, 512, 2048
P = 128
FLOPS = 2 * B * NQ * NSLOT * D

F32 = mybir.dt.float32
BF16 = mybir.dt.bfloat16
I32 = mybir.dt.int32
U32 = mybir.dt.uint32
U16 = mybir.dt.uint16
U8 = mybir.dt.uint8
E4M3 = mybir.dt.float8_e4m3fn_x4
E5M2 = mybir.dt.float8_e5m2_x4


def tile_attend_dk_kernel(tc, g, qm, offs, out):
    nc = tc.nc
    with ExitStack() as ctx:
        held = ctx.enter_context(tc.tile_pool(name="held", bufs=1))
        psum = ctx.enter_context(tc.psum_pool(name="psum", bufs=1))

        def tile(shape, dtype, name):
            return held.tile(shape, dtype, name=name, align_bytes=64)

        offsets = held.tile([P, B * NSLOT // 16], U16, name="offsets")

        def load(raw, src):
            nc.sync.dma_start(out=raw, in_=src.rearrange("(p j) w -> p j w", j=4))

        def quantise(codes, scales, fmt, grouped):
            nc.vector.quantize_mx(out=codes.bitcast(fmt), scales=scales, in_=grouped.rearrange("p w j -> p (w j)"))

        pieces = [(0, 128), (128, 256), (256, 512)]
        q_raw = [[tile([P, 4, c1 - c0], F32, "q_raw_%d_%d" % (k, b)) for b in range(B)] for k, (c0, c1) in enumerate(pieces)]
        q_grp = [tile([P, B, P, 4], BF16, "q_grp_%d" % k) for k in range(2)]
        q_codes = [tile([P, B, P], U32, "q_codes_0"), held.tile([P, B, P], U32, name="q_codes_1", tag="shared", align_bytes=64), tile([P, B, 2 * P], U32, "q_codes_2")]
        q_scales = [tile([P, B, c1 - c0], U8, "q_scales_%d" % k) for k, (c0, c1) in enumerate(pieces)]
        spans = [[(0, 512)], [(0, 256), (256, 512)]]
        g_raw = [[tile([P, 4, c1 - c0], F32, "g_raw_%d_%d" % (b, h)) for h, (c0, c1) in enumerate(spans[b])] for b in range(B)]
        g_grp = [tile([P, NSLOT, 4], BF16, "g_grp_%d" % b) for b in range(B)]
        g_codes = [tile([P, NSLOT], U32, "g_codes_%d" % b) for b in range(B)]
        g_scales = [tile([P, NSLOT], U8, "g_scales_%d" % b) for b in range(B)]
        windows = [tile([P, T], F32, "window_%d" % m) for m in range(D // P)]

        def load_g(b, h):
            c0, c1 = spans[b][h]
            load(g_raw[b][h][:], g[b, :, c0:c1])

        def load_q(k, b):
            c0, c1 = pieces[k]
            load(q_raw[k][b][:], qm[b, :, c0:c1])

        def quantise_g(b, h):
            c0, c1 = spans[b][h]
            quantise(g_codes[b][:, c0:c1], g_scales[b][:, c0:c1], E5M2, g_grp[b][:, c0:c1, :])

        def group_g(b, h, n):
            c0, c1 = spans[b][h]
            raw = g_raw[b][h]
            nc.vector.tensor_copy(out=g_grp[b][:, c0:c0 + n, :].rearrange("p (c i) j -> p c j i", i=4), in_=raw[:, :, 0:n].rearrange("p j (c i) -> p c j i", i=4))
            nc.scalar.copy(out=g_grp[b][:, c0 + n:c1, :].rearrange("p (c i) j -> p c j i", i=4), in_=raw[:, :, n:c1 - c0].rearrange("p j (c i) -> p c j i", i=4))

        def group_q(k, b, n):
            w = pieces[k][1] - pieces[k][0]
            if n:
                nc.vector.tensor_copy(out=q_grp[k][:, b, 0:n, :].rearrange("p (c i) j -> p c j i", i=4), in_=q_raw[k][b][:, :, 0:n].rearrange("p j (c i) -> p c j i", i=4))
            if n < w:
                nc.scalar.copy(out=q_grp[k][:, b, n:w, :].rearrange("p (c i) j -> p c j i", i=4), in_=q_raw[k][b][:, :, n:w].rearrange("p j (c i) -> p c j i", i=4))

        def quantise_q(k, b):
            quantise(q_codes[k][:, b, :], q_scales[k][:, b, :], E4M3, q_grp[k][:, b, :, :])

        accs = {}
        staged = {}

        def product(m, b):
            k = min(m, 2)
            c0 = m * P - pieces[k][0]
            acc = psum.tile([P, NSLOT], F32, name="acc_%d_%d" % (m, b))
            nc.tensor.matmul_mx(
                out=acc[:],
                lhsT=q_codes[k][:, b, c0:c0 + P].bitcast(E4M3),
                lhsT_scale=q_scales[k][:, b, c0:c0 + P],
                rhs=g_codes[b][:].bitcast(E5M2),
                rhs_scale=g_scales[b][:],
                start=True,
                stop=True,
            )
            accs[m, b] = acc

        def copy_out(m, b):
            if b == 0:
                staged[m] = tile([P, B, NSLOT], F32, "vals_%d" % m)
            nc.scalar.copy(out=staged[m][:, b, :], in_=accs[m, b][:])

        def scatter(m, b):
            nc.vector.tensor_copy(windows[m][:].indirect(offsets[:, b * 32:b * 32 + 32]), staged[m][:, b, :])

        def store(m):
            nc.sync.dma_start(out=out[m * P:m * P + P, :], in_=windows[m][:])

        load_g(0, 0)
        load_g(1, 0)
        load_q(0, 0)
        load_q(0, 1)
        load_g(1, 1)
        load_q(1, 0)
        load_q(1, 1)
        nc.sync.dma_start(offsets[:], offs)
        load_q(2, 0)
        load_q(2, 1)
        for m in range(D // P):
            engine = nc.gpsimd if m == 3 else nc.vector
            engine.memset(windows[m][:].bitcast(I32), 0)

        group_g(0, 0, 256)
        group_g(1, 0, 128)
        quantise_g(0, 0)
        group_q(0, 0, 0)
        quantise_q(0, 0)
        product(0, 0)
        quantise_g(1, 0)
        group_q(0, 1, 0)
        group_g(1, 1, 128)
        quantise_q(0, 1)
        quantise_g(1, 1)
        product(0, 1)
        for b in range(B):
            group_q(1, b, 64)
        copy_out(0, 0)
        for b in range(B):
            quantise_q(1, b)
        scatter(0, 0)
        for b in range(B):
            product(1, b)
        copy_out(0, 1)
        scatter(0, 1)
        store(0)
        q_grp.append(held.tile([P, B, 2 * P, 4], BF16, name="q_grp_2", tag="shared", align_bytes=64))
        for b in range(B):
            group_q(2, b, 256 - 256 * b)
            quantise_q(2, b)
        for m in (1, 2, 3):
            for b in range(B):
                if m > 1:
                    product(m, b)
                copy_out(m, b)
                scatter(m, b)
            store(m)
